import numpy as np
import ml_dtypes

BF16 = ml_dtypes.bfloat16


def bf(x):
    return np.asarray(x, np.float32).astype(BF16)


def f32(x):
    return np.asarray(x, np.float32)


def f64(x):
    return np.asarray(x).astype(np.float64)


def striped(idx):
    return np.tile(idx.reshape(-1, 16).T, (8, 1))


S, K, M, N = 512, 512, 256, 64


def setup_inputs():
    return {"base": bf(np.random.standard_normal((M, S))), "x": bf(np.random.standard_normal((K, N))), "w": bf(np.random.standard_normal((K, M)) / np.sqrt(K)), "s": f32(0.5 + np.random.random_sample((M, 1))), "b": f32(0.5 * np.random.standard_normal((M, 1))), "offs": striped(np.random.permutation(S)[:N])}


def reference(base, x, w, s, b, offs):
    idx = offs[:16].T.reshape(-1)
    z = f64(base).copy()
    z[:, idx] += f64(w).T @ f64(x)
    return z * f64(s) + f64(b)

@@ -1,0 +1,69 @@
+import concourse.mybir as mybir
+from concourse.masks import make_identity
+
+P = 128
+S = 512
+K = 512
+M = 256
+N = 64
+K_BLOCKS = K // P
+M_BLOCKS = M // P
+
+FLOPS = 2 * K * M * N
+
+BF16 = mybir.dt.bfloat16
+F32 = mybir.dt.float32
+U16 = mybir.dt.uint16
+MULT = mybir.AluOpType.mult
+ADD = mybir.AluOpType.add
+IDENTITY = mybir.ActivationFunctionType.Identity
+
+
+def tile_scatter_matmul_kernel(tc, base, x, w, s, b, offs, out):
+    nc = tc.nc
+    with (
+        tc.tile_pool(name="held", bufs=1) as held,
+        tc.psum_pool(name="banks", bufs=1) as banks,
+    ):
+        offsets = held.tile([P, N // 16], U16, name="offsets")
+        nc.sync.dma_start(offsets[:], offs)
+
+        base_rows = [held.tile([P, S], BF16, name="base_rows%d" % a) for a in range(M_BLOCKS)]
+        nc.sync.dma_start(base_rows[0][:], base[0:P, :])
+        nc.scalar.dma_start(base_rows[1][:], base[P : 2 * P, :])
+
+        x_rows = held.tile([P, K_BLOCKS, N], BF16, name="x_rows")
+        nc.sync.dma_start(x_rows[:], x.rearrange("(p c) n -> p c n", c=K_BLOCKS))
+        w_rows = held.tile([P, K_BLOCKS, M], BF16, name="w_rows")
+        nc.scalar.dma_start(w_rows[:], w.rearrange("(p c) m -> p c m", c=K_BLOCKS))
+
+        gain = held.tile([P, M_BLOCKS], F32, name="gain")
+        shift = held.tile([P, M_BLOCKS], F32, name="shift")
+        with nc.allow_non_contiguous_dma(reason="one float32 to a partition, 256 in all"):
+            nc.sync.dma_start(gain[:], s.rearrange("(a p) o -> p (a o)", p=P))
+            nc.scalar.dma_start(shift[:], b.rearrange("(a p) o -> p (a o)", p=P))
+
+        ident = held.tile([P, P], BF16, name="ident")
+        make_identity(nc, ident[:])
+
+        windows = [banks.tile([P, S], F32, name="window%d" % a) for a in range(M_BLOCKS)]
+        for a in range(M_BLOCKS):
+            nc.tensor.matmul(windows[a][:], ident[:], base_rows[a][:], start=True, stop=False)
+
+        for a in range(M_BLOCKS):
+            for c in range(K_BLOCKS):
+                nc.tensor.matmul(
+                    windows[a][:].indirect(offsets[:]),
+                    w_rows[:, c, a * P : (a + 1) * P],
+                    x_rows[:, c, :],
+                    start=False,
+                    stop=(c == K_BLOCKS - 1),
+                )
+
+        result0 = held.tile([P, S], F32, name="result0")
+        nc.vector.tensor_scalar(result0[:], windows[0][:], gain[:, 0:1], shift[:, 0:1], MULT, ADD)
+        nc.sync.dma_start(out[0:P, :], result0[:])
+
+        result1 = held.tile([P, S], F32, name="result1")
+        nc.scalar.activation(result1[:], windows[1][:], IDENTITY, bias=shift[:, 1:2], scale=gain[:, 1:2])
+        nc.scalar.dma_start(out[P : 2 * P, :], result1[:])

@@ -8,6 +8,8 @@ M = 256
 N = 64
 K_BLOCKS = K // P
 M_BLOCKS = M // P
+HALF = S // 2
+WARM_UPS = 4
 
 FLOPS = 2 * K * M * N
 
@@ -25,23 +27,34 @@ def tile_scatter_matmul_kernel(tc, base, x, w, s, b, offs, out):
         tc.tile_pool(name="held", bufs=1) as held,
         tc.psum_pool(name="banks", bufs=1) as banks,
     ):
-        offsets = held.tile([P, N // 16], U16, name="offsets")
-        nc.sync.dma_start(offsets[:], offs)
-
         base_rows = [held.tile([P, S], BF16, name="base_rows%d" % a) for a in range(M_BLOCKS)]
         nc.sync.dma_start(base_rows[0][:], base[0:P, :])
         nc.scalar.dma_start(base_rows[1][:], base[P : 2 * P, :])
 
+        offsets = held.tile([P, N // 16], U16, name="offsets")
+        nc.sync.dma_start(offsets[:], offs)
+
         x_rows = held.tile([P, K_BLOCKS, N], BF16, name="x_rows")
-        nc.sync.dma_start(x_rows[:], x.rearrange("(p c) n -> p c n", c=K_BLOCKS))
+        nc.scalar.dma_start(x_rows[:], x.rearrange("(p c) n -> p c n", c=K_BLOCKS))
+        w_by_partition = w.rearrange("(p c) m -> p c m", c=K_BLOCKS)
         w_rows = held.tile([P, K_BLOCKS, M], BF16, name="w_rows")
-        nc.scalar.dma_start(w_rows[:], w.rearrange("(p c) m -> p c m", c=K_BLOCKS))
+        nc.sync.dma_start(w_rows[:, 0 : K_BLOCKS // 2, :], w_by_partition[:, 0 : K_BLOCKS // 2, :])
+        nc.scalar.dma_start(w_rows[:, K_BLOCKS // 2 :, :], w_by_partition[:, K_BLOCKS // 2 :, :])
 
         gain = held.tile([P, M_BLOCKS], F32, name="gain")
         shift = held.tile([P, M_BLOCKS], F32, name="shift")
         with nc.allow_non_contiguous_dma(reason="one float32 to a partition, 256 in all"):
             nc.sync.dma_start(gain[:], s.rearrange("(a p) o -> p (a o)", p=P))
             nc.scalar.dma_start(shift[:], b.rearrange("(a p) o -> p (a o)", p=P))
+
+        zeros = held.tile([P, P], BF16, name="zeros")
+        nc.gpsimd.memset(zeros[:], 0.0)
+        idle_column = held.tile([P, 1], F32, name="idle_column")
+        nc.scalar.activation(idle_column[:], zeros[:, 0:1], IDENTITY)
+        idle_bank = banks.tile([P, S // P, P], F32, name="idle_bank")
+        zeros_repeated = zeros[:].unsqueeze(1).to_broadcast([P, S // P, P])
+        for i in range(WARM_UPS):
+            nc.tensor.matmul(idle_bank[:], zeros[:], zeros_repeated, start=True, stop=True)
 
         ident = held.tile([P, P], BF16, name="ident")
         make_identity(nc, ident[:])
@@ -60,10 +73,24 @@ def tile_scatter_matmul_kernel(tc, base, x, w, s, b, offs, out):
                     stop=(c == K_BLOCKS - 1),
                 )
 
-        result0 = held.tile([P, S], F32, name="result0")
-        nc.vector.tensor_scalar(result0[:], windows[0][:], gain[:, 0:1], shift[:, 0:1], MULT, ADD)
-        nc.sync.dma_start(out[0:P, :], result0[:])
-
-        result1 = held.tile([P, S], F32, name="result1")
-        nc.scalar.activation(result1[:], windows[1][:], IDENTITY, bias=shift[:, 1:2], scale=gain[:, 1:2])
-        nc.scalar.dma_start(out[P : 2 * P, :], result1[:])
+        for a in range(M_BLOCKS):
+            result = held.tile([P, S], F32, name="result%d" % a)
+            for left in range(0, S, HALF):
+                if a == 0:
+                    nc.vector.tensor_scalar(
+                        result[:, left : left + HALF],
+                        windows[a][:, left : left + HALF],
+                        gain[:, a : a + 1],
+                        shift[:, a : a + 1],
+                        MULT,
+                        ADD,
+                    )
+                else:
+                    nc.scalar.activation(
+                        result[:, left : left + HALF],
+                        windows[a][:, left : left + HALF],
+                        IDENTITY,
+                        bias=shift[:, a : a + 1],
+                        scale=gain[:, a : a + 1],
+                    )
+                nc.sync.dma_start(out[a * P : (a + 1) * P, left : left + HALF], result[:, left : left + HALF])

@@ -9,7 +9,6 @@ N = 64
 K_BLOCKS = K // P
 M_BLOCKS = M // P
 HALF = S // 2
-WARM_UPS = 4
 
 FLOPS = 2 * K * M * N
 
@@ -47,14 +46,10 @@ def tile_scatter_matmul_kernel(tc, base, x, w, s, b, offs, out):
             nc.sync.dma_start(gain[:], s.rearrange("(a p) o -> p (a o)", p=P))
             nc.scalar.dma_start(shift[:], b.rearrange("(a p) o -> p (a o)", p=P))
 
-        zeros = held.tile([P, P], BF16, name="zeros")
+        zeros = held.tile([P, 1], F32, name="zeros")
         nc.gpsimd.memset(zeros[:], 0.0)
         idle_column = held.tile([P, 1], F32, name="idle_column")
-        nc.scalar.activation(idle_column[:], zeros[:, 0:1], IDENTITY)
-        idle_bank = banks.tile([P, S // P, P], F32, name="idle_bank")
-        zeros_repeated = zeros[:].unsqueeze(1).to_broadcast([P, S // P, P])
-        for i in range(WARM_UPS):
-            nc.tensor.matmul(idle_bank[:], zeros[:], zeros_repeated, start=True, stop=True)
+        nc.scalar.activation(idle_column[:], zeros[:], IDENTITY)
 
         ident = held.tile([P, P], BF16, name="ident")
         make_identity(nc, ident[:])

@@ -9,6 +9,7 @@ N = 64
 K_BLOCKS = K // P
 M_BLOCKS = M // P
 HALF = S // 2
+WARM_UPS = 3
 
 FLOPS = 2 * K * M * N
 
@@ -46,10 +47,14 @@ def tile_scatter_matmul_kernel(tc, base, x, w, s, b, offs, out):
             nc.sync.dma_start(gain[:], s.rearrange("(a p) o -> p (a o)", p=P))
             nc.scalar.dma_start(shift[:], b.rearrange("(a p) o -> p (a o)", p=P))
 
-        zeros = held.tile([P, 1], F32, name="zeros")
+        zeros = held.tile([P, P], BF16, name="zeros")
         nc.gpsimd.memset(zeros[:], 0.0)
         idle_column = held.tile([P, 1], F32, name="idle_column")
-        nc.scalar.activation(idle_column[:], zeros[:], IDENTITY)
+        nc.scalar.activation(idle_column[:], zeros[:, 0:1], IDENTITY)
+        idle_bank = banks.tile([P, S // P, P], F32, name="idle_bank")
+        zeros_repeated = zeros[:].unsqueeze(1).to_broadcast([P, S // P, P])
+        for i in range(WARM_UPS):
+            nc.tensor.matmul(idle_bank[:], zeros[:], zeros_repeated, start=True, stop=True)
 
         ident = held.tile([P, P], BF16, name="ident")
         make_identity(nc, ident[:])

@@ -48,7 +48,7 @@ def tile_scatter_matmul_kernel(tc, base, x, w, s, b, offs, out):
             nc.scalar.dma_start(shift[:], b.rearrange("(a p) o -> p (a o)", p=P))
 
         zeros = held.tile([P, P], BF16, name="zeros")
-        nc.gpsimd.memset(zeros[:], 0.0)
+        nc.vector.memset(zeros[:], 0.0)
         idle_column = held.tile([P, 1], F32, name="idle_column")
         nc.scalar.activation(idle_column[:], zeros[:, 0:1], IDENTITY)
         idle_bank = banks.tile([P, S // P, P], F32, name="idle_bank")
@@ -57,7 +57,8 @@ def tile_scatter_matmul_kernel(tc, base, x, w, s, b, offs, out):
             nc.tensor.matmul(idle_bank[:], zeros[:], zeros_repeated, start=True, stop=True)
 
         ident = held.tile([P, P], BF16, name="ident")
-        make_identity(nc, ident[:])
+        nc.vector.memset(ident[:], 0.0)
+        make_identity(nc, ident[:], nomemset=True)
 
         windows = [banks.tile([P, S], F32, name="window%d" % a) for a in range(M_BLOCKS)]
         for a in range(M_BLOCKS):

@@ -29,23 +29,23 @@ def tile_scatter_matmul_kernel(tc, base, x, w, s, b, offs, out):
     ):
         base_rows = [held.tile([P, S], BF16, name="base_rows%d" % a) for a in range(M_BLOCKS)]
         nc.sync.dma_start(base_rows[0][:], base[0:P, :])
-        nc.scalar.dma_start(base_rows[1][:], base[P : 2 * P, :])
+        nc.sync.dma_start(base_rows[1][:], base[P : 2 * P, :])
 
         offsets = held.tile([P, N // 16], U16, name="offsets")
         nc.sync.dma_start(offsets[:], offs)
 
         x_rows = held.tile([P, K_BLOCKS, N], BF16, name="x_rows")
-        nc.scalar.dma_start(x_rows[:], x.rearrange("(p c) n -> p c n", c=K_BLOCKS))
+        nc.sync.dma_start(x_rows[:], x.rearrange("(p c) n -> p c n", c=K_BLOCKS))
         w_by_partition = w.rearrange("(p c) m -> p c m", c=K_BLOCKS)
         w_rows = held.tile([P, K_BLOCKS, M], BF16, name="w_rows")
         nc.sync.dma_start(w_rows[:, 0 : K_BLOCKS // 2, :], w_by_partition[:, 0 : K_BLOCKS // 2, :])
-        nc.scalar.dma_start(w_rows[:, K_BLOCKS // 2 :, :], w_by_partition[:, K_BLOCKS // 2 :, :])
+        nc.sync.dma_start(w_rows[:, K_BLOCKS // 2 :, :], w_by_partition[:, K_BLOCKS // 2 :, :])
 
         gain = held.tile([P, M_BLOCKS], F32, name="gain")
         shift = held.tile([P, M_BLOCKS], F32, name="shift")
         with nc.allow_non_contiguous_dma(reason="one float32 to a partition, 256 in all"):
             nc.sync.dma_start(gain[:], s.rearrange("(a p) o -> p (a o)", p=P))
-            nc.scalar.dma_start(shift[:], b.rearrange("(a p) o -> p (a o)", p=P))
+            nc.sync.dma_start(shift[:], b.rearrange("(a p) o -> p (a o)", p=P))
 
         zeros = held.tile([P, P], BF16, name="zeros")
         nc.vector.memset(zeros[:], 0.0)

@@ -10,6 +10,8 @@ K_BLOCKS = K // P
 M_BLOCKS = M // P
 HALF = S // 2
 WARM_UPS = 3
+SQUARE = 32
+SQUARES = P // SQUARE
 
 FLOPS = 2 * K * M * N
 
@@ -41,14 +43,16 @@ def tile_scatter_matmul_kernel(tc, base, x, w, s, b, offs, out):
         nc.sync.dma_start(w_rows[:, 0 : K_BLOCKS // 2, :], w_by_partition[:, 0 : K_BLOCKS // 2, :])
         nc.sync.dma_start(w_rows[:, K_BLOCKS // 2 :, :], w_by_partition[:, K_BLOCKS // 2 :, :])
 
-        gain = held.tile([P, M_BLOCKS], F32, name="gain")
-        shift = held.tile([P, M_BLOCKS], F32, name="shift")
-        with nc.allow_non_contiguous_dma(reason="one float32 to a partition, 256 in all"):
-            nc.sync.dma_start(gain[:], s.rearrange("(a p) o -> p (a o)", p=P))
-            nc.sync.dma_start(shift[:], b.rearrange("(a p) o -> p (a o)", p=P))
-
         zeros = held.tile([P, P], BF16, name="zeros")
         nc.vector.memset(zeros[:], 0.0)
+        as_rows = held.tile([P, SQUARES * SQUARE], F32, name="as_rows", align_bytes=64)
+        nc.vector.memset(as_rows[:], 0.0)
+        for values, first in ((s, 0), (b, M_BLOCKS * SQUARE)):
+            nc.scalar.dma_start(
+                as_rows[0:P:SQUARE, first : first + M_BLOCKS * SQUARE].rearrange("q (a j) -> q a j", a=M_BLOCKS),
+                values.rearrange("(a q j) o -> q a (j o)", a=M_BLOCKS, q=SQUARES),
+            )
+
         idle_column = held.tile([P, 1], F32, name="idle_column")
         nc.scalar.activation(idle_column[:], zeros[:, 0:1], IDENTITY)
         idle_bank = banks.tile([P, S // P, P], F32, name="idle_bank")
@@ -59,6 +63,11 @@ def tile_scatter_matmul_kernel(tc, base, x, w, s, b, offs, out):
         ident = held.tile([P, P], BF16, name="ident")
         nc.vector.memset(ident[:], 0.0)
         make_identity(nc, ident[:], nomemset=True)
+
+        as_columns = held.tile([P, SQUARES * SQUARE], F32, name="as_columns", align_bytes=64)
+        nc.vector.transpose(as_columns[:], as_rows[:])
+        gain = [as_columns[:, a * SQUARE : a * SQUARE + 1] for a in range(M_BLOCKS)]
+        shift = [as_columns[:, (M_BLOCKS + a) * SQUARE : (M_BLOCKS + a) * SQUARE + 1] for a in range(M_BLOCKS)]
 
         windows = [banks.tile([P, S], F32, name="window%d" % a) for a in range(M_BLOCKS)]
         for a in range(M_BLOCKS):
@@ -81,8 +90,8 @@ def tile_scatter_matmul_kernel(tc, base, x, w, s, b, offs, out):
                     nc.vector.tensor_scalar(
                         result[:, left : left + HALF],
                         windows[a][:, left : left + HALF],
-                        gain[:, a : a + 1],
-                        shift[:, a : a + 1],
+                        gain[a],
+                        shift[a],
                         MULT,
                         ADD,
                     )
@@ -91,7 +100,7 @@ def tile_scatter_matmul_kernel(tc, base, x, w, s, b, offs, out):
                         result[:, left : left + HALF],
                         windows[a][:, left : left + HALF],
                         IDENTITY,
-                        bias=shift[:, a : a + 1],
-                        scale=gain[:, a : a + 1],
+                        bias=shift[a],
+                        scale=gain[a],
                     )
                 nc.sync.dma_start(out[a * P : (a + 1) * P, left : left + HALF], result[:, left : left + HALF])

@@ -86,7 +86,7 @@ def tile_scatter_matmul_kernel(tc, base, x, w, s, b, offs, out):
         for a in range(M_BLOCKS):
             result = held.tile([P, S], F32, name="result%d" % a)
             for left in range(0, S, HALF):
-                if a == 0:
+                if a == M_BLOCKS - 1:
                     nc.vector.tensor_scalar(
                         result[:, left : left + HALF],
                         windows[a][:, left : left + HALF],

@@ -86,7 +86,16 @@ def tile_scatter_matmul_kernel(tc, base, x, w, s, b, offs, out):
         for a in range(M_BLOCKS):
             result = held.tile([P, S], F32, name="result%d" % a)
             for left in range(0, S, HALF):
-                if a == M_BLOCKS - 1:
+                if a == 0:
+                    nc.scalar.activation(
+                        result[:, left : left + HALF],
+                        windows[a][:, left : left + HALF],
+                        IDENTITY,
+                        bias=shift[a],
+                        scale=gain[a],
+                    )
+                    nc.scalar.dma_start(out[a * P : (a + 1) * P, left : left + HALF], result[:, left : left + HALF])
+                else:
                     nc.vector.tensor_scalar(
                         result[:, left : left + HALF],
                         windows[a][:, left : left + HALF],
@@ -95,12 +104,4 @@ def tile_scatter_matmul_kernel(tc, base, x, w, s, b, offs, out):
                         MULT,
                         ADD,
                     )
-                else:
-                    nc.scalar.activation(
-                        result[:, left : left + HALF],
-                        windows[a][:, left : left + HALF],
-                        IDENTITY,
-                        bias=shift[a],
-                        scale=gain[a],
-                    )
-                nc.sync.dma_start(out[a * P : (a + 1) * P, left : left + HALF], result[:, left : left + HALF])
+                    nc.sync.dma_start(out[a * P : (a + 1) * P, left : left + HALF], result[:, left : left + HALF])

@@ -94,7 +94,7 @@ def tile_scatter_matmul_kernel(tc, base, x, w, s, b, offs, out):
                         bias=shift[a],
                         scale=gain[a],
                     )
-                    nc.scalar.dma_start(out[a * P : (a + 1) * P, left : left + HALF], result[:, left : left + HALF])
+                    nc.sync.dma_start(out[a * P : (a + 1) * P, left : left + HALF], result[:, left : left + HALF])
                 else:
                     nc.vector.tensor_scalar(
                         result[:, left : left + HALF],
@@ -104,4 +104,4 @@ def tile_scatter_matmul_kernel(tc, base, x, w, s, b, offs, out):
                         MULT,
                         ADD,
                     )
-                    nc.sync.dma_start(out[a * P : (a + 1) * P, left : left + HALF], result[:, left : left + HALF])
+                    nc.scalar.dma_start(out[a * P : (a + 1) * P, left : left + HALF], result[:, left : left + HALF])

import concourse.mybir as mybir
from concourse.masks import make_identity

P = 128
S = 512
K = 512
M = 256
N = 64
K_BLOCKS = K // P
M_BLOCKS = M // P
HALF = S // 2
WARM_UPS = 3
SQUARE = 32
SQUARES = P // SQUARE

FLOPS = 2 * K * M * N

BF16 = mybir.dt.bfloat16
F32 = mybir.dt.float32
U16 = mybir.dt.uint16
MULT = mybir.AluOpType.mult
ADD = mybir.AluOpType.add
IDENTITY = mybir.ActivationFunctionType.Identity


def tile_scatter_matmul_kernel(tc, base, x, w, s, b, offs, out):
    nc = tc.nc
    with (
        tc.tile_pool(name="held", bufs=1) as held,
        tc.psum_pool(name="banks", bufs=1) as banks,
    ):
        base_rows = [held.tile([P, S], BF16, name="base_rows%d" % a) for a in range(M_BLOCKS)]
        nc.sync.dma_start(base_rows[0][:], base[0:P, :])
        nc.sync.dma_start(base_rows[1][:], base[P : 2 * P, :])

        offsets = held.tile([P, N // 16], U16, name="offsets")
        nc.sync.dma_start(offsets[:], offs)

        x_rows = held.tile([P, K_BLOCKS, N], BF16, name="x_rows")
        nc.sync.dma_start(x_rows[:], x.rearrange("(p c) n -> p c n", c=K_BLOCKS))
        w_by_partition = w.rearrange("(p c) m -> p c m", c=K_BLOCKS)
        w_rows = held.tile([P, K_BLOCKS, M], BF16, name="w_rows")
        nc.sync.dma_start(w_rows[:, 0 : K_BLOCKS // 2, :], w_by_partition[:, 0 : K_BLOCKS // 2, :])
        nc.sync.dma_start(w_rows[:, K_BLOCKS // 2 :, :], w_by_partition[:, K_BLOCKS // 2 :, :])

        zeros = held.tile([P, P], BF16, name="zeros")
        nc.vector.memset(zeros[:], 0.0)
        as_rows = held.tile([P, SQUARES * SQUARE], F32, name="as_rows", align_bytes=64)
        nc.vector.memset(as_rows[:], 0.0)
        for values, first in ((s, 0), (b, M_BLOCKS * SQUARE)):
            nc.scalar.dma_start(
                as_rows[0:P:SQUARE, first : first + M_BLOCKS * SQUARE].rearrange("q (a j) -> q a j", a=M_BLOCKS),
                values.rearrange("(a q j) o -> q a (j o)", a=M_BLOCKS, q=SQUARES),
            )

        idle_column = held.tile([P, 1], F32, name="idle_column")
        nc.scalar.activation(idle_column[:], zeros[:, 0:1], IDENTITY)
        idle_bank = banks.tile([P, S // P, P], F32, name="idle_bank")
        zeros_repeated = zeros[:].unsqueeze(1).to_broadcast([P, S // P, P])
        for i in range(WARM_UPS):
            nc.tensor.matmul(idle_bank[:], zeros[:], zeros_repeated, start=True, stop=True)

        ident = held.tile([P, P], BF16, name="ident")
        nc.vector.memset(ident[:], 0.0)
        make_identity(nc, ident[:], nomemset=True)

        as_columns = held.tile([P, SQUARES * SQUARE], F32, name="as_columns", align_bytes=64)
        nc.vector.transpose(as_columns[:], as_rows[:])
        gain = [as_columns[:, a * SQUARE : a * SQUARE + 1] for a in range(M_BLOCKS)]
        shift = [as_columns[:, (M_BLOCKS + a) * SQUARE : (M_BLOCKS + a) * SQUARE + 1] for a in range(M_BLOCKS)]

        windows = [banks.tile([P, S], F32, name="window%d" % a) for a in range(M_BLOCKS)]
        for a in range(M_BLOCKS):
            nc.tensor.matmul(windows[a][:], ident[:], base_rows[a][:], start=True, stop=False)

        for a in range(M_BLOCKS):
            for c in range(K_BLOCKS):
                nc.tensor.matmul(
                    windows[a][:].indirect(offsets[:]),
                    w_rows[:, c, a * P : (a + 1) * P],
                    x_rows[:, c, :],
                    start=False,
                    stop=(c == K_BLOCKS - 1),
                )

        for a in range(M_BLOCKS):
            result = held.tile([P, S], F32, name="result%d" % a)
            for left in range(0, S, HALF):
                if a == 0:
                    nc.scalar.activation(
                        result[:, left : left + HALF],
                        windows[a][:, left : left + HALF],
                        IDENTITY,
                        bias=shift[a],
                        scale=gain[a],
                    )
                    nc.sync.dma_start(out[a * P : (a + 1) * P, left : left + HALF], result[:, left : left + HALF])
                else:
                    nc.vector.tensor_scalar(
                        result[:, left : left + HALF],
                        windows[a][:, left : left + HALF],
                        gain[a],
                        shift[a],
                        MULT,
                        ADD,
                    )
                    nc.scalar.dma_start(out[a * P : (a + 1) * P, left : left + HALF], result[:, left : left + HALF])
